import numpy as np
import ml_dtypes


def mxq(x, axis, fmt="e4m3"):
    dtype, down = {"e4m3": (ml_dtypes.float8_e4m3fn, 7), "e5m2": (ml_dtypes.float8_e5m2, 14)}[fmt]
    v = np.moveaxis(np.asarray(x, np.float32).astype(ml_dtypes.bfloat16).astype(np.float64), axis, -1)
    blocks = v.reshape(v.shape[:-1] + (-1, 32))
    amax = np.abs(blocks).max(-1, keepdims=True)
    byte = np.maximum(np.where(amax > 0, np.frexp(amax)[1] - 1 + 127, 0) - down, 1)
    scale = np.exp2(byte - 127.0)
    codes = (blocks / scale).astype(np.float32).astype(dtype).astype(np.float64)
    return np.moveaxis((codes * scale).reshape(v.shape), -1, axis)


WIDE = False


def mx_kscale(k):
    if not WIDE:
        return np.ones(k)
    levels = np.array([10, -10, 5, -5, 0])
    if k % 512:
        return np.exp2(np.random.permutation(np.resize(levels, k // 32))).repeat(32)
    a = np.empty((k // 512, 16))
    for p in range(k // 512):
        a[p, :8] = np.random.permutation(np.resize(levels, 8))
        for g in range(8):
            far = levels[np.abs(levels - a[p, g]) >= 10]
            a[p, g + 8] = far[np.random.randint(len(far))]
    return np.exp2(a.ravel()).repeat(32)


BF16 = ml_dtypes.bfloat16


def bf(x):
    return np.asarray(x, np.float32).astype(BF16)


def f64(x):
    return np.asarray(x).astype(np.float64)


N, M, D, E, P = 8192, 512, 512, 512, 256


def exp_kernel(a, b):
    scale = np.sqrt(a.shape[-1])
    return np.exp((mxq(a, 1, "e4m3") @ mxq(b.T, 0, "e4m3")) / scale)


def double_centre(l):
    mr = np.mean(l, axis=1)
    mc = np.mean(l, axis=0)
    mm = np.mean(mr)
    return l - mr[:, None] - mc[None, :] + mm


def draw0():
    s, g, t = mx_kscale(D), mx_kscale(E), mx_kscale(M)
    y = 0.8 * np.random.standard_normal((N, E)) + 0.3 * np.random.standard_normal((1, E))
    v = 0.8 * np.random.standard_normal((M, E)) + 0.3 * np.random.standard_normal((1, E))
    return {
        "x": bf(np.random.standard_normal((N, D)) * 0.8 * s),
        "u": bf(np.random.standard_normal((M, D)) * 0.8 / s),
        "y": bf(y * g),
        "v": bf(v / g),
        "r": bf((1.0 + 0.1 * np.random.standard_normal(M)) * t),
        "z": bf(np.random.standard_normal((M, P)) / t[:, None]),
    }


def core(x, u, y, v, r, z):
    k = exp_kernel(f64(x), f64(u))
    l = exp_kernel(f64(y), f64(v))
    lc = double_centre(l)
    a = k * lc * f64(r)[None, :]
    return (mxq(a, 1, "e4m3") @ mxq(f64(z), 0, "e4m3")) / np.sqrt(z.shape[0])


def e4m3fn_bytes(y):
    return np.clip(np.asarray(y, np.float64), -448.0, 448.0).astype(np.float32).astype(ml_dtypes.float8_e4m3fn).view(np.uint8)


def e4m3fn_values(b):
    return np.asarray(b, np.uint8).view(ml_dtypes.float8_e4m3fn).astype(np.float64)


def setup_inputs():
    d = draw0()
    x0 = np.asarray(d['y']).astype(np.float64)
    s = (np.max(np.abs(x0), axis=(0,), keepdims=True) / 448.0).astype(np.float32)
    out = {}
    for k, v in d.items():
        if k == 'y':
            out['y_bytes'] = e4m3fn_bytes(x0 / s.astype(np.float64))
            out['y_scale'] = s
        else:
            out[k] = v
    return out


def reference(x, u, y_bytes, y_scale, v, r, z):
    return core(x, u, e4m3fn_values(y_bytes) * y_scale.astype(np.float64), v, r, z)

@@ -1,0 +1,382 @@
+import math
+from contextlib import ExitStack
+
+import concourse.mybir as mybir
+from concourse.masks import make_identity
+
+N, M, D, Z = 8192, 512, 512, 256
+FLOPS = 2 * N * M * (D + D + Z)
+
+F32 = mybir.dt.float32
+BF16 = mybir.dt.bfloat16
+U32 = mybir.dt.uint32
+U8 = mybir.dt.uint8
+FP8 = mybir.dt.float8_e4m3fn
+FP8X4 = mybir.dt.float8_e4m3fn_x4
+ALU = mybir.AluOpType
+ACT = mybir.ActivationFunctionType
+AX = mybir.AxisListType
+
+P = 128
+T = 4
+CHUNK = 512
+CHUNKS = N // CHUNK
+ROOT = 1.0 / math.sqrt(512.0)
+
+
+def tile_hsicexpkernelgrad_t_kernel(tc, x, u, y_bytes, y_scale, v, r, z, out):
+    nc = tc.nc
+    x_rows = x.rearrange("(c p b) k -> c p (b k)", p=P, b=T)
+    y_rows = y_bytes.rearrange("(c p b) k -> c p (b k)", p=P, b=T)
+    out_rows = out.rearrange("(c p b) n -> c p (b n)", p=P, b=T)
+
+    with ExitStack() as ctx:
+        keep = ctx.enter_context(tc.tile_pool(name="keep", bufs=1))
+        work = ctx.enter_context(tc.tile_pool(name="work", bufs=2))
+        psum = ctx.enter_context(tc.psum_pool(name="psum", bufs=2))
+        ctx.enter_context(tc.manual_schedule())
+
+        ident = keep.tile([P, P], F32, name="ident")
+        scale_in = keep.tile([P, T], F32, name="scale_in")
+        scale_row = keep.tile([P, 2 * D], F32, name="scale_row")
+        r_in = keep.tile([P, T], BF16, name="r_in")
+        r_abs = keep.tile([P, T], F32, name="r_abs")
+        r_log = keep.tile([P, T], F32, name="r_log")
+        r_sign = keep.tile([P, T], F32, name="r_sign")
+        z_in = keep.tile([P, T, Z], BF16, name="z_in")
+        col_sums = keep.tile([P, T, CHUNKS], F32, name="col_sums")
+        row_sums = keep.tile([P, T * CHUNKS], F32, name="row_sums")
+        row_means = keep.tile([P, T * CHUNKS], F32, name="row_means")
+
+        loads, scaled, grouped, codes, banks, lmat, kmat, outs = {}, {}, {}, {}, {}, {}, {}, {}
+
+        def load_x(key, rows):
+            loads[key] = work.tile([P, T * D], BF16, name="x_in", tag="x_in", bufs=3)
+            nc.sync.dma_start(out=loads[key][:], in_=rows)
+
+        def load_y(c):
+            loads["y", c] = work.tile([P, T * D], U8, name="y_codes_in", tag="y_codes_in", bufs=4)
+            nc.sync.dma_start(out=loads["y", c][:], in_=y_rows[c])
+
+        def widen_y(c):
+            scaled["y", c] = work.tile([P, T * D], BF16, name="y_bf", tag="y_bf", bufs=2)
+            for h in range(2):
+                cols = slice(2 * D * h, 2 * D * (h + 1))
+                nc.vector.tensor_tensor(
+                    out=scaled["y", c][:, cols], in0=loads["y", c][:, cols].bitcast(FP8), in1=scale_row[:], op=ALU.mult
+                )
+
+        def turn(key, src):
+            words = src[:].bitcast(F32)
+            for h in range(2):
+                bank = psum.tile([P, 2, 2 * P], F32, name="turned", tag="turned", bufs=2)
+                banks[key, h] = bank
+                for b in (0, 1):
+                    for w in range(2):
+                        first = (2 * h + b) * (D // 2)
+                        nc.tensor.transpose(
+                            bank[:, w, P * b : P * (b + 1)], words[:, first + w : first + D // 2 : 2], ident[:]
+                        )
+
+        def group(key):
+            grouped[key] = work.tile([P, T * CHUNK], BF16, name="grouped", tag="grouped", bufs=3, align_bytes=64)
+            words = grouped[key][:].bitcast(F32).rearrange("p (n w) -> p n w", w=2)
+            for h in range(2):
+                nc.scalar.copy(
+                    out=words[:, 2 * P * h : 2 * P * (h + 1), :], in_=banks[key, h][:].rearrange("p w n -> p n w")
+                )
+
+        def quantize(key, pool, tag, bufs):
+            code = pool.tile([P, CHUNK], U32, name="code" + tag, tag="code" + tag, bufs=bufs, align_bytes=64)
+            scale = pool.tile([P, CHUNK], U8, name="scale" + tag, tag="scale" + tag, bufs=bufs, align_bytes=64)
+            nc.vector.quantize_mx(out=code[:].bitcast(FP8X4), scales=scale[:], in_=grouped[key][:])
+            codes[key] = (code, scale)
+
+        def logits(key, weight, t):
+            bank = psum.tile([P, CHUNK], F32, name="bank", tag="bank", bufs=4)
+            w_code, w_scale = codes[weight]
+            code, scale = codes[key]
+            cols = slice(P * t, P * (t + 1))
+            nc.tensor.matmul_mx(
+                out=bank[:],
+                lhsT=w_code[:, cols].bitcast(FP8X4),
+                lhsT_scale=w_scale[:, cols],
+                rhs=code[:].bitcast(FP8X4),
+                rhs_scale=scale[:],
+                start=True,
+                stop=True,
+            )
+            banks[key, "logits", t] = bank
+
+        def exp_l(c):
+            lmat[c] = keep.tile([P, T, CHUNK], F32, name="l", tag="l", bufs=CHUNKS)
+            for t in range(T):
+                nc.scalar.activation(
+                    out=lmat[c][:, t, :],
+                    in_=banks[("y", c), "logits", t][:],
+                    func=ACT.Exp,
+                    scale=ROOT,
+                    accum_out=col_sums[:, t, c : c + 1],
+                )
+
+        def exp_k(c):
+            kmat[c] = work.tile([P, T, CHUNK], F32, name="k", tag="k", bufs=2)
+            for t in range(T):
+                nc.scalar.activation(
+                    out=kmat[c][:, t, :],
+                    in_=banks[("x", c), "logits", t][:],
+                    func=ACT.Exp,
+                    scale=ROOT,
+                    bias=r_log[:, t : t + 1],
+                )
+
+        def slot_sums(c):
+            bank = psum.tile([P, T, P], F32, name="side", tag="side", bufs=2)
+            for b in range(T):
+                for t in range(T):
+                    nc.tensor.matmul(
+                        bank[:, b, :],
+                        lhsT=lmat[c][:, t, P * b : P * (b + 1)],
+                        rhs=ident[:],
+                        start=(t == 0),
+                        stop=(t == T - 1),
+                        is_transpose=True,
+                    )
+            banks["sums", c] = bank
+
+        def reduce_rows(c):
+            nc.vector.tensor_reduce(
+                out=row_sums[:, T * c : T * (c + 1)], in_=banks["sums", c][:], axis=AX.X, op=ALU.add
+            )
+
+        def scale_means(c0, c1):
+            cols = slice(T * c0, T * c1)
+            nc.vector.tensor_scalar(
+                out=row_means[:, cols], in0=row_sums[:, cols], scalar1=1.0 / M, scalar2=None, op0=ALU.mult
+            )
+
+        def spread_means(c):
+            bank = psum.tile([P, T, P], F32, name="side", tag="side", bufs=2)
+            for b in range(T):
+                col = T * c + b
+                nc.tensor.transpose(bank[:, b, :], row_means[:, col : col + 1].to_broadcast([P, P]), ident[:])
+            banks["means", c] = bank
+
+        def centre(c):
+            means = banks["means", c][:].rearrange("p b i -> p (b i)")
+            for t in range(T):
+                nc.vector.scalar_tensor_tensor(
+                    out=lmat[c][:, t, :],
+                    in0=lmat[c][:, t, :],
+                    scalar=col_shift[:, t : t + 1],
+                    in1=means,
+                    op0=ALU.add,
+                    op1=ALU.subtract,
+                )
+
+        def combine(c):
+            key = ("a", c)
+            grouped[key] = work.tile([P, T * CHUNK], BF16, name="a_bf", tag="a_bf", bufs=2, align_bytes=64)
+            nc.vector.tensor_tensor(
+                out=grouped[key][:].rearrange("p (n i t) -> p n t i", t=T, i=4),
+                in0=lmat[c][:].rearrange("p t (n i) -> p n t i", i=4),
+                in1=kmat[c][:].rearrange("p t (n i) -> p n t i", i=4),
+                op=ALU.mult,
+            )
+
+        def product(c):
+            code, scale = codes["a", c]
+            z_code, z_scale = codes["z"]
+            for h in range(2):
+                bank = psum.tile([P, 2, Z], F32, name="bank", tag="bank", bufs=4)
+                for b in range(2):
+                    cols = slice(P * (2 * h + b), P * (2 * h + b + 1))
+                    nc.tensor.matmul_mx(
+                        out=bank[:, b, :],
+                        lhsT=code[:, cols].bitcast(FP8X4),
+                        lhsT_scale=scale[:, cols],
+                        rhs=z_code[:].bitcast(FP8X4),
+                        rhs_scale=z_scale[:],
+                        start=True,
+                        stop=True,
+                    )
+                banks["out", c, h] = bank
+
+        def finish(c):
+            outs[c] = work.tile([P, T * Z], F32, name="out_sb", tag="out_sb", bufs=2)
+            for h in range(2):
+                nc.scalar.activation(
+                    out=outs[c][:, 2 * Z * h : 2 * Z * (h + 1)],
+                    in_=banks["out", c, h][:].rearrange("p b n -> p (b n)"),
+                    func=ACT.Copy,
+                    scale=ROOT,
+                )
+
+        def store(c):
+            nc.sync.dma_start(out=out_rows[c], in_=outs[c][:])
+
+        def have(c):
+            return 0 <= c < CHUNKS
+
+        nc.sync.dma_start(out=scale_in[:], in_=y_scale.rearrange("o (p t) -> p (o t)", t=T))
+        nc.sync.dma_start(out=r_in[:], in_=r.rearrange("(p t) -> p t", t=T))
+        load_y(0)
+        load_x("v", v.rearrange("(p b) k -> p (b k)", b=T))
+        load_y(1)
+        load_y(2)
+        load_x("u", u.rearrange("(p b) k -> p (b k)", b=T))
+        nc.sync.dma_start(out=z_in[:], in_=z.rearrange("(p t) n -> p t n", t=T))
+        make_identity(nc, ident[:])
+
+        nc.vector.scalar_tensor_tensor(
+            out=r_abs[:], in0=r_in[:], scalar=-1.0, in1=r_in[:], op0=ALU.mult, op1=ALU.max
+        )
+        nc.vector.tensor_scalar(
+            out=r_abs[:], in0=r_abs[:], scalar1=2.0**-120, scalar2=2.0**120, op0=ALU.max, op1=ALU.min
+        )
+        factors = keep.tile([P, 3, T], F32, name="factors")
+        nc.vector.tensor_scalar(
+            out=factors[:, 0, :], in0=r_abs[:], scalar1=2.0**-60, scalar2=2.0**60, op0=ALU.max, op1=ALU.min
+        )
+        nc.vector.tensor_scalar(
+            out=factors[:, 1, :], in0=r_abs[:], scalar1=2.0**-60, scalar2=1.0, op0=ALU.mult, op1=ALU.max
+        )
+        nc.vector.tensor_scalar(
+            out=factors[:, 2, :], in0=r_abs[:], scalar1=2.0**60, scalar2=1.0, op0=ALU.mult, op1=ALU.min
+        )
+        logs = keep.tile([P, 3, T], F32, name="logs")
+        nc.scalar.activation(out=logs[:], in_=factors[:], func=ACT.Ln)
+
+        scale_bank = psum.tile([P, T, P], F32, name="side", tag="side", bufs=2)
+        for t in range(T):
+            nc.tensor.transpose(scale_bank[:, t, :], scale_in[:, t : t + 1].to_broadcast([P, P]), ident[:])
+        for h in range(2):
+            nc.vector.tensor_copy(
+                out=scale_row[:, D * h : D * (h + 1)].rearrange("p (q t) -> p q t", t=T),
+                in_=scale_bank[:].rearrange("p t q -> p q t"),
+            )
+
+        def kernel_l_step(s):
+            if have(s):
+                for t in range(T):
+                    logits(("y", s), "v", t)
+            if have(s + 2):
+                turn(("y", s + 2), scaled["y", s + 2])
+            if have(s - 1):
+                slot_sums(s - 1)
+            if have(s):
+                exp_l(s)
+            if have(s + 2):
+                group(("y", s + 2))
+            if have(s - 2):
+                reduce_rows(s - 2)
+            if have(s + 1):
+                quantize(("y", s + 1), work, "w", 3)
+            if have(s + 3):
+                widen_y(s + 3)
+            if 3 <= s + 4 < CHUNKS:
+                load_y(s + 4)
+
+        kernel_l_step(-3)
+        turn("v", loads["v"])
+        group("v")
+        nc.vector.tensor_reduce(out=r_log[:], in_=logs[:].rearrange("p f t -> p t f"), axis=AX.X, op=ALU.add)
+        kernel_l_step(-2)
+        quantize("v", keep, "v", 1)
+        r_exp = keep.tile([P, T], F32, name="r_exp")
+        nc.scalar.activation(out=r_exp[:], in_=r_log[:], func=ACT.Exp)
+        kernel_l_step(-1)
+        nc.vector.reciprocal(out=r_exp[:], in_=r_exp[:])
+        nc.vector.tensor_tensor(out=r_exp[:], in0=r_exp[:], in1=r_abs[:], op=ALU.mult)
+        nc.vector.scalar_tensor_tensor(
+            out=r_log[:], in0=r_exp[:], scalar=-1.0, in1=r_log[:], op0=ALU.add, op1=ALU.add
+        )
+        nc.vector.tensor_scalar(
+            out=r_sign[:], in0=r_in[:], scalar1=0.0, scalar2=2.0, op0=ALU.is_ge, op1=ALU.mult
+        )
+        nc.vector.tensor_scalar(out=r_sign[:], in0=r_sign[:], scalar1=-1.0, scalar2=None, op0=ALU.add)
+        for s in range(CHUNKS):
+            kernel_l_step(s)
+            if s == 2:
+                turn("u", loads["u"])
+                group("u")
+            if s == 3:
+                quantize("u", keep, "u", 1)
+            if s == 4:
+                z_grouped = keep.tile([P, Z, T], BF16, name="z_grouped", align_bytes=64)
+                nc.vector.tensor_tensor(
+                    out=z_grouped[:],
+                    in0=z_in[:].rearrange("p t n -> p n t"),
+                    in1=r_sign[:].unsqueeze(1).to_broadcast([P, Z, T]),
+                    op=ALU.mult,
+                )
+            if s == 5:
+                z_code = keep.tile([P, Z], U32, name="z_code", align_bytes=64)
+                z_scale = keep.tile([P, Z], U8, name="z_scale", align_bytes=64)
+                nc.vector.quantize_mx(
+                    out=z_code[:].bitcast(FP8X4), scales=z_scale[:], in_=z_grouped[:].rearrange("p n t -> p (n t)")
+                )
+                codes["z"] = (z_code, z_scale)
+            if s == 10:
+                scale_means(0, 8)
+            if 10 <= s < 13:
+                load_x(("x", s - 10), x_rows[s - 10])
+            if s >= 14:
+                turn(("x", s - 14), loads["x", s - 14])
+                group(("x", s - 14))
+                load_x(("x", s - 11), x_rows[s - 11])
+            if s == 15:
+                quantize(("x", 0), work, "w", 3)
+                spread_means(0)
+        kernel_l_step(CHUNKS)
+
+        col_sum = keep.tile([P, T], F32, name="col_sum")
+        part_sum = keep.tile([P, 1], F32, name="part_sum")
+        total = keep.tile([P, 1], F32, name="total")
+        mean = keep.tile([P, 1], F32, name="mean")
+        col_shift = keep.tile([P, T], F32, name="col_shift")
+        nc.vector.tensor_reduce(out=part_sum[:], in_=col_sums[:], axis=AX.XY, op=ALU.add)
+        nc.vector.tensor_reduce(out=col_sum[:], in_=col_sums[:], axis=AX.X, op=ALU.add)
+        total_bank = psum.tile([P, P], F32, name="bank", tag="bank", bufs=4)
+        nc.tensor.transpose(total_bank[:], part_sum[:].to_broadcast([P, P]), ident[:])
+        quantize(("x", 1), work, "w", 3)
+        nc.vector.tensor_reduce(out=total[:], in_=total_bank[:], axis=AX.X, op=ALU.add)
+        reduce_rows(CHUNKS - 1)
+        nc.vector.tensor_scalar(
+            out=mean[:], in0=total[:], scalar1=1.0 / (N * M), scalar2=None, op0=ALU.mult
+        )
+        scale_means(8, CHUNKS)
+        nc.vector.tensor_scalar(
+            out=col_shift[:], in0=col_sum[:], scalar1=-1.0 / N, scalar2=mean[:], op0=ALU.mult, op1=ALU.add
+        )
+
+        def kernel_k_step(s):
+            if have(s - 1):
+                product(s - 1)
+            if have(s + 1):
+                for t in range(T):
+                    logits(("x", s + 1), "u", t)
+            if have(s + 3):
+                turn(("x", s + 3), loads["x", s + 3])
+            if have(s + 2):
+                spread_means(s + 2)
+            if have(s - 1):
+                finish(s - 1)
+                store(s - 1)
+            if have(s + 1):
+                exp_k(s + 1)
+            if have(s + 3):
+                group(("x", s + 3))
+            if have(s):
+                combine(s)
+            if have(s + 1):
+                centre(s + 1)
+            if have(s):
+                quantize(("a", s), work, "a", 2)
+            if have(s + 2) and s >= 0:
+                quantize(("x", s + 2), work, "w", 3)
+            if have(s + 6):
+                load_x(("x", s + 6), x_rows[s + 6])
+
+        for s in range(-1, CHUNKS + 1):
+            kernel_k_step(s)

@@ -22,6 +22,10 @@ T = 4
 CHUNK = 512
 CHUNKS = N // CHUNK
 ROOT = 1.0 / math.sqrt(512.0)
+X_AHEAD = 12
+X_FIRST_STEP = 2
+X_BOTH = 11
+POOL_COLS = 208
 
 
 def tile_hsicexpkernelgrad_t_kernel(tc, x, u, y_bytes, y_scale, v, r, z, out):
@@ -43,9 +47,8 @@ def tile_hsicexpkernelgrad_t_kernel(tc, x, u, y_bytes, y_scale, v, r, z, out):
         r_abs = keep.tile([P, T], F32, name="r_abs")
         r_log = keep.tile([P, T], F32, name="r_log")
         r_sign = keep.tile([P, T], F32, name="r_sign")
-        z_in = keep.tile([P, T, Z], BF16, name="z_in")
+        z_in = work.tile([P, T, Z], BF16, name="z_in", tag="x_in", bufs=3)
         col_sums = keep.tile([P, T, CHUNKS], F32, name="col_sums")
-        row_sums = keep.tile([P, T * CHUNKS], F32, name="row_sums")
         row_means = keep.tile([P, T * CHUNKS], F32, name="row_means")
 
         loads, scaled, grouped, codes, banks, lmat, kmat, outs = {}, {}, {}, {}, {}, {}, {}, {}
@@ -55,21 +58,22 @@ def tile_hsicexpkernelgrad_t_kernel(tc, x, u, y_bytes, y_scale, v, r, z, out):
             nc.sync.dma_start(out=loads[key][:], in_=rows)
 
         def load_y(c):
-            loads["y", c] = work.tile([P, T * D], U8, name="y_codes_in", tag="y_codes_in", bufs=4)
+            loads["y", c] = work.tile([P, T * D], U8, name="y_codes_in", tag="y_codes_in", bufs=3)
             nc.sync.dma_start(out=loads["y", c][:], in_=y_rows[c])
 
-        def widen_y(c):
-            scaled["y", c] = work.tile([P, T * D], BF16, name="y_bf", tag="y_bf", bufs=2)
-            for h in range(2):
+        def widen_y(c, halves=(0, 1)):
+            if 0 in halves:
+                scaled["y", c] = work.tile([P, T * D], BF16, name="y_bf", tag="rows", bufs=2)
+            for h in halves:
                 cols = slice(2 * D * h, 2 * D * (h + 1))
                 nc.vector.tensor_tensor(
                     out=scaled["y", c][:, cols], in0=loads["y", c][:, cols].bitcast(FP8), in1=scale_row[:], op=ALU.mult
                 )
 
-        def turn(key, src):
+        def turn(key, src, tag="turned"):
             words = src[:].bitcast(F32)
             for h in range(2):
-                bank = psum.tile([P, 2, 2 * P], F32, name="turned", tag="turned", bufs=2)
+                bank = psum.tile([P, 2, 2 * P], F32, name="turned", tag=tag, bufs=2)
                 banks[key, h] = bank
                 for b in (0, 1):
                     for w in range(2):
@@ -78,17 +82,16 @@ def tile_hsicexpkernelgrad_t_kernel(tc, x, u, y_bytes, y_scale, v, r, z, out):
                             bank[:, w, P * b : P * (b + 1)], words[:, first + w : first + D // 2 : 2], ident[:]
                         )
 
-        def group(key):
-            grouped[key] = work.tile([P, T * CHUNK], BF16, name="grouped", tag="grouped", bufs=3, align_bytes=64)
+        def group(key, halves=(nc.scalar.copy, nc.scalar.copy)):
+            grouped[key] = work.tile([P, T * CHUNK], BF16, name="grouped", tag="grouped", bufs=4, align_bytes=64)
             words = grouped[key][:].bitcast(F32).rearrange("p (n w) -> p n w", w=2)
-            for h in range(2):
-                nc.scalar.copy(
-                    out=words[:, 2 * P * h : 2 * P * (h + 1), :], in_=banks[key, h][:].rearrange("p w n -> p n w")
-                )
+            for h, copy in enumerate(halves):
+                copy(out=words[:, 2 * P * h : 2 * P * (h + 1), :], in_=banks[key, h][:].rearrange("p w n -> p n w"))
 
         def quantize(key, pool, tag, bufs):
-            code = pool.tile([P, CHUNK], U32, name="code" + tag, tag="code" + tag, bufs=bufs, align_bytes=64)
-            scale = pool.tile([P, CHUNK], U8, name="scale" + tag, tag="scale" + tag, bufs=bufs, align_bytes=64)
+            width = grouped[key].shape[1] // T
+            code = pool.tile([P, width], U32, name="code" + tag, tag="code" + tag, bufs=bufs, align_bytes=64)
+            scale = pool.tile([P, width], U8, name="scale" + tag, tag="scale" + tag, bufs=bufs, align_bytes=64)
             nc.vector.quantize_mx(out=code[:].bitcast(FP8X4), scales=scale[:], in_=grouped[key][:])
             codes[key] = (code, scale)
 
@@ -131,7 +134,7 @@ def tile_hsicexpkernelgrad_t_kernel(tc, x, u, y_bytes, y_scale, v, r, z, out):
                 )
 
         def slot_sums(c):
-            bank = psum.tile([P, T, P], F32, name="side", tag="side", bufs=2)
+            bank = psum.tile([P, T, P], F32, name="sums", tag="turned", bufs=2)
             for b in range(T):
                 for t in range(T):
                     nc.tensor.matmul(
@@ -145,15 +148,15 @@ def tile_hsicexpkernelgrad_t_kernel(tc, x, u, y_bytes, y_scale, v, r, z, out):
             banks["sums", c] = bank
 
         def reduce_rows(c):
-            nc.vector.tensor_reduce(
-                out=row_sums[:, T * c : T * (c + 1)], in_=banks["sums", c][:], axis=AX.X, op=ALU.add
-            )
-
-        def scale_means(c0, c1):
-            cols = slice(T * c0, T * c1)
-            nc.vector.tensor_scalar(
-                out=row_means[:, cols], in0=row_sums[:, cols], scalar1=1.0 / M, scalar2=None, op0=ALU.mult
-            )
+            for b in range(T):
+                spare = work.tile([P, P], F32, name="spare", tag="spare", bufs=1)
+                nc.scalar.activation(
+                    out=spare[:],
+                    in_=banks["sums", c][:, b, :],
+                    func=ACT.Copy,
+                    scale=1.0 / M,
+                    accum_out=row_means[:, T * c + b : T * c + b + 1],
+                )
 
         def spread_means(c):
             bank = psum.tile([P, T, P], F32, name="side", tag="side", bufs=2)
@@ -176,13 +179,16 @@ def tile_hsicexpkernelgrad_t_kernel(tc, x, u, y_bytes, y_scale, v, r, z, out):
 
         def combine(c):
             key = ("a", c)
-            grouped[key] = work.tile([P, T * CHUNK], BF16, name="a_bf", tag="a_bf", bufs=2, align_bytes=64)
-            nc.vector.tensor_tensor(
-                out=grouped[key][:].rearrange("p (n i t) -> p n t i", t=T, i=4),
-                in0=lmat[c][:].rearrange("p t (n i) -> p n t i", i=4),
-                in1=kmat[c][:].rearrange("p t (n i) -> p n t i", i=4),
-                op=ALU.mult,
-            )
+            grouped[key] = work.tile([P, T * CHUNK], BF16, name="a_bf", tag="grouped", bufs=4, align_bytes=64)
+            mine = (CHUNK - (POOL_COLS if c < CHUNKS - 1 else 0)) // 4
+            parts = ((nc.gpsimd, slice(mine, CHUNK // 4)), (nc.vector, slice(0, mine)))
+            for engine, cols in parts[c // (CHUNKS - 1) :]:
+                engine.tensor_tensor(
+                    out=grouped[key][:].rearrange("p (n i t) -> p n t i", t=T, i=4)[:, cols],
+                    in0=lmat[c][:].rearrange("p t (n i) -> p n t i", i=4)[:, cols],
+                    in1=kmat[c][:].rearrange("p t (n i) -> p n t i", i=4)[:, cols],
+                    op=ALU.mult,
+                )
 
         def product(c):
             code, scale = codes["a", c]
@@ -203,7 +209,7 @@ def tile_hsicexpkernelgrad_t_kernel(tc, x, u, y_bytes, y_scale, v, r, z, out):
                 banks["out", c, h] = bank
 
         def finish(c):
-            outs[c] = work.tile([P, T * Z], F32, name="out_sb", tag="out_sb", bufs=2)
+            outs[c] = work.tile([P, T * Z], F32, name="out_sb", tag="rows", bufs=2)
             for h in range(2):
                 nc.scalar.activation(
                     out=outs[c][:, 2 * Z * h : 2 * Z * (h + 1)],
@@ -226,7 +232,10 @@ def tile_hsicexpkernelgrad_t_kernel(tc, x, u, y_bytes, y_scale, v, r, z, out):
         load_y(2)
         load_x("u", u.rearrange("(p b) k -> p (b k)", b=T))
         nc.sync.dma_start(out=z_in[:], in_=z.rearrange("(p t) n -> p t n", t=T))
+        one = keep.tile([P, 1], F32, name="one")
+        nc.gpsimd.memset(one[:], 1.0)
         make_identity(nc, ident[:])
+        nc.scalar.activation(out=one[:], in_=one[:], func=ACT.Ln)
 
         nc.vector.scalar_tensor_tensor(
             out=r_abs[:], in0=r_in[:], scalar=-1.0, in1=r_in[:], op0=ALU.mult, op1=ALU.max
@@ -234,6 +243,16 @@ def tile_hsicexpkernelgrad_t_kernel(tc, x, u, y_bytes, y_scale, v, r, z, out):
         nc.vector.tensor_scalar(
             out=r_abs[:], in0=r_abs[:], scalar1=2.0**-120, scalar2=2.0**120, op0=ALU.max, op1=ALU.min
         )
+
+        scale_bank = psum.tile([P, T, P], F32, name="side", tag="side", bufs=2)
+        for t in range(T):
+            nc.tensor.transpose(scale_bank[:, t, :], scale_in[:, t : t + 1].to_broadcast([P, P]), ident[:])
+        for h in range(2):
+            nc.vector.tensor_copy(
+                out=scale_row[:, D * h : D * (h + 1)].rearrange("p (q t) -> p q t", t=T),
+                in_=scale_bank[:].rearrange("p t q -> p q t"),
+            )
+
         factors = keep.tile([P, 3, T], F32, name="factors")
         nc.vector.tensor_scalar(
             out=factors[:, 0, :], in0=r_abs[:], scalar1=2.0**-60, scalar2=2.0**60, op0=ALU.max, op1=ALU.min
@@ -246,137 +265,143 @@ def tile_hsicexpkernelgrad_t_kernel(tc, x, u, y_bytes, y_scale, v, r, z, out):
         )
         logs = keep.tile([P, 3, T], F32, name="logs")
         nc.scalar.activation(out=logs[:], in_=factors[:], func=ACT.Ln)
-
-        scale_bank = psum.tile([P, T, P], F32, name="side", tag="side", bufs=2)
-        for t in range(T):
-            nc.tensor.transpose(scale_bank[:, t, :], scale_in[:, t : t + 1].to_broadcast([P, P]), ident[:])
-        for h in range(2):
-            nc.vector.tensor_copy(
-                out=scale_row[:, D * h : D * (h + 1)].rearrange("p (q t) -> p q t", t=T),
-                in_=scale_bank[:].rearrange("p t q -> p q t"),
-            )
+        nc.scalar.activation(out=one[:], in_=one[:], func=ACT.Exp)
 
         def kernel_l_step(s):
+            new_x = s - X_FIRST_STEP
             if have(s):
                 for t in range(T):
                     logits(("y", s), "v", t)
             if have(s + 2):
                 turn(("y", s + 2), scaled["y", s + 2])
-            if have(s - 1):
-                slot_sums(s - 1)
+            if 0 <= new_x < X_AHEAD:
+                turn(("x", new_x), loads["x", new_x], "side")
             if have(s):
                 exp_l(s)
             if have(s + 2):
                 group(("y", s + 2))
-            if have(s - 2):
-                reduce_rows(s - 2)
             if have(s + 1):
-                quantize(("y", s + 1), work, "w", 3)
+                quantize(("y", s + 1), work, "w", 2)
+            if 0 <= new_x - 1 < X_AHEAD:
+                quantize(("x", new_x - 1), work, "x", X_AHEAD + 1)
             if have(s + 3):
                 widen_y(s + 3)
-            if 3 <= s + 4 < CHUNKS:
+            if 0 <= new_x < X_AHEAD:
+                copy = nc.scalar.copy if new_x < X_BOTH else nc.vector.tensor_copy
+                group(("x", new_x), (copy, nc.vector.tensor_copy))
+            if s + 4 < CHUNKS:
                 load_y(s + 4)
+            if 0 <= new_x + 2 < CHUNKS and new_x + 2 < X_AHEAD + 3:
+                load_x(("x", new_x + 2), x_rows[new_x + 2])
 
-        kernel_l_step(-3)
+        widen_y(0)
         turn("v", loads["v"])
         group("v")
-        nc.vector.tensor_reduce(out=r_log[:], in_=logs[:].rearrange("p f t -> p t f"), axis=AX.X, op=ALU.add)
-        kernel_l_step(-2)
+        turn(("y", 0), scaled["y", 0])
+        group(("y", 0))
+        widen_y(1, (0,))
         quantize("v", keep, "v", 1)
-        r_exp = keep.tile([P, T], F32, name="r_exp")
-        nc.scalar.activation(out=r_exp[:], in_=r_log[:], func=ACT.Exp)
-        kernel_l_step(-1)
-        nc.vector.reciprocal(out=r_exp[:], in_=r_exp[:])
-        nc.vector.tensor_tensor(out=r_exp[:], in0=r_exp[:], in1=r_abs[:], op=ALU.mult)
-        nc.vector.scalar_tensor_tensor(
-            out=r_log[:], in0=r_exp[:], scalar=-1.0, in1=r_log[:], op0=ALU.add, op1=ALU.add
-        )
-        nc.vector.tensor_scalar(
-            out=r_sign[:], in0=r_in[:], scalar1=0.0, scalar2=2.0, op0=ALU.is_ge, op1=ALU.mult
-        )
-        nc.vector.tensor_scalar(out=r_sign[:], in0=r_sign[:], scalar1=-1.0, scalar2=None, op0=ALU.add)
+        quantize(("y", 0), work, "w", 2)
+        widen_y(1, (1,))
+        turn(("y", 1), scaled["y", 1])
+        group(("y", 1))
+        widen_y(2)
+        load_y(3)
         for s in range(CHUNKS):
             kernel_l_step(s)
+            if s == 1:
+                r_exp = keep.tile([P, T], F32, name="r_exp")
+                nc.gpsimd.tensor_tensor(out=r_log[:], in0=logs[:, 0, :], in1=logs[:, 1, :], op=ALU.add)
+                nc.gpsimd.tensor_tensor(out=r_log[:], in0=r_log[:], in1=logs[:, 2, :], op=ALU.add)
+                nc.scalar.activation(out=r_exp[:], in_=r_log[:], func=ACT.Exp, scale=-1.0)
+                nc.gpsimd.tensor_tensor(out=r_exp[:], in0=r_exp[:], in1=r_abs[:], op=ALU.mult)
+                nc.gpsimd.tensor_scalar(out=r_exp[:], in0=r_exp[:], scalar1=1.0, scalar2=None, op0=ALU.subtract)
+                nc.gpsimd.tensor_tensor(out=r_log[:], in0=r_log[:], in1=r_exp[:], op=ALU.add)
+                nc.gpsimd.tensor_scalar(
+                    out=r_sign[:], in0=r_in[:], scalar1=0.0, scalar2=2.0, op0=ALU.is_ge, op1=ALU.mult
+                )
+                nc.gpsimd.tensor_scalar(out=r_sign[:], in0=r_sign[:], scalar1=1.0, scalar2=None, op0=ALU.subtract)
             if s == 2:
                 turn("u", loads["u"])
                 group("u")
             if s == 3:
                 quantize("u", keep, "u", 1)
             if s == 4:
-                z_grouped = keep.tile([P, Z, T], BF16, name="z_grouped", align_bytes=64)
+                grouped["z"] = work.tile([P, Z * T], BF16, name="z_grouped", tag="grouped", bufs=4, align_bytes=64)
                 nc.vector.tensor_tensor(
-                    out=z_grouped[:],
+                    out=grouped["z"][:].rearrange("p (n t) -> p n t", t=T),
                     in0=z_in[:].rearrange("p t n -> p n t"),
                     in1=r_sign[:].unsqueeze(1).to_broadcast([P, Z, T]),
                     op=ALU.mult,
                 )
             if s == 5:
-                z_code = keep.tile([P, Z], U32, name="z_code", align_bytes=64)
-                z_scale = keep.tile([P, Z], U8, name="z_scale", align_bytes=64)
-                nc.vector.quantize_mx(
-                    out=z_code[:].bitcast(FP8X4), scales=z_scale[:], in_=z_grouped[:].rearrange("p n t -> p (n t)")
-                )
-                codes["z"] = (z_code, z_scale)
-            if s == 10:
-                scale_means(0, 8)
-            if 10 <= s < 13:
-                load_x(("x", s - 10), x_rows[s - 10])
-            if s >= 14:
-                turn(("x", s - 14), loads["x", s - 14])
-                group(("x", s - 14))
-                load_x(("x", s - 11), x_rows[s - 11])
-            if s == 15:
-                quantize(("x", 0), work, "w", 3)
-                spread_means(0)
-        kernel_l_step(CHUNKS)
+                quantize("z", keep, "z", 1)
+            if s >= CHUNKS - 3:
+                slot_sums(s - CHUNKS + 3)
+            if s >= CHUNKS - 2:
+                reduce_rows(s - CHUNKS + 2)
 
-        col_sum = keep.tile([P, T], F32, name="col_sum")
+        col_mean = keep.tile([P, T], F32, name="col_mean")
         part_sum = keep.tile([P, 1], F32, name="part_sum")
         total = keep.tile([P, 1], F32, name="total")
-        mean = keep.tile([P, 1], F32, name="mean")
         col_shift = keep.tile([P, T], F32, name="col_shift")
         nc.vector.tensor_reduce(out=part_sum[:], in_=col_sums[:], axis=AX.XY, op=ALU.add)
-        nc.vector.tensor_reduce(out=col_sum[:], in_=col_sums[:], axis=AX.X, op=ALU.add)
-        total_bank = psum.tile([P, P], F32, name="bank", tag="bank", bufs=4)
+        nc.vector.tensor_reduce(out=col_mean[:], in_=col_sums[:], axis=AX.X, op=ALU.add)
+        nc.vector.tensor_scalar(
+            out=col_mean[:], in0=col_mean[:], scalar1=1.0 / N, scalar2=None, op0=ALU.mult
+        )
+        total_bank = psum.tile([P, P], F32, name="total_bank", tag="side", bufs=2)
+        for t in range(T):
+            logits(("x", 0), "u", t)
         nc.tensor.transpose(total_bank[:], part_sum[:].to_broadcast([P, P]), ident[:])
-        quantize(("x", 1), work, "w", 3)
         nc.vector.tensor_reduce(out=total[:], in_=total_bank[:], axis=AX.X, op=ALU.add)
-        reduce_rows(CHUNKS - 1)
-        nc.vector.tensor_scalar(
-            out=mean[:], in0=total[:], scalar1=1.0 / (N * M), scalar2=None, op0=ALU.mult
+        nc.vector.scalar_tensor_tensor(
+            out=col_shift[:],
+            in0=total[:].to_broadcast([P, T]),
+            scalar=1.0 / (N * M),
+            in1=col_mean[:],
+            op0=ALU.mult,
+            op1=ALU.subtract,
         )
-        scale_means(8, CHUNKS)
-        nc.vector.tensor_scalar(
-            out=col_shift[:], in0=col_sum[:], scalar1=-1.0 / N, scalar2=mean[:], op0=ALU.mult, op1=ALU.add
-        )
+        spread_means(0)
+        exp_k(0)
+        spread_means(1)
+        if X_FIRST_STEP + X_AHEAD == CHUNKS:
+            quantize(("x", X_AHEAD - 1), work, "x", X_AHEAD + 1)
+        reduce_rows(2)
+        centre(0)
 
         def kernel_k_step(s):
-            if have(s - 1):
-                product(s - 1)
             if have(s + 1):
                 for t in range(T):
                     logits(("x", s + 1), "u", t)
-            if have(s + 3):
+            if have(s - 2):
+                product(s - 2)
+            if have(s + 3) and s + 3 >= X_AHEAD:
                 turn(("x", s + 3), loads["x", s + 3])
+            if have(s + 3):
+                slot_sums(s + 3)
             if have(s + 2):
                 spread_means(s + 2)
-            if have(s - 1):
-                finish(s - 1)
-                store(s - 1)
             if have(s + 1):
                 exp_k(s + 1)
-            if have(s + 3):
+            if have(s - 2):
+                finish(s - 2)
+                store(s - 2)
+            if have(s + 3) and s + 3 >= X_AHEAD:
                 group(("x", s + 3))
-            if have(s):
-                combine(s)
+            if have(s + 3):
+                reduce_rows(s + 3)
             if have(s + 1):
                 centre(s + 1)
             if have(s):
-                quantize(("a", s), work, "a", 2)
-            if have(s + 2) and s >= 0:
-                quantize(("x", s + 2), work, "w", 3)
-            if have(s + 6):
+                combine(s)
+            if have(s + 2) and s + 2 >= X_AHEAD:
+                quantize(("x", s + 2), work, "x", X_AHEAD + 1)
+            if have(s - 1):
+                quantize(("a", s - 1), work, "w", 2)
+            if have(s + 6) and s + 6 >= X_AHEAD + 3:
                 load_x(("x", s + 6), x_rows[s + 6])
 
-        for s in range(-1, CHUNKS + 1):
+        for s in range(CHUNKS + 2):
             kernel_k_step(s)

@@ -22,7 +22,7 @@ T = 4
 CHUNK = 512
 CHUNKS = N // CHUNK
 ROOT = 1.0 / math.sqrt(512.0)
-X_AHEAD = 12
+X_AHEAD = 14
 X_FIRST_STEP = 2
 X_BOTH = 11
 POOL_COLS = 208
@@ -42,7 +42,6 @@ def tile_hsicexpkernelgrad_t_kernel(tc, x, u, y_bytes, y_scale, v, r, z, out):
 
         ident = keep.tile([P, P], F32, name="ident")
         scale_in = keep.tile([P, T], F32, name="scale_in")
-        scale_row = keep.tile([P, 2 * D], F32, name="scale_row")
         r_in = keep.tile([P, T], BF16, name="r_in")
         r_abs = keep.tile([P, T], F32, name="r_abs")
         r_log = keep.tile([P, T], F32, name="r_log")
@@ -61,14 +60,12 @@ def tile_hsicexpkernelgrad_t_kernel(tc, x, u, y_bytes, y_scale, v, r, z, out):
             loads["y", c] = work.tile([P, T * D], U8, name="y_codes_in", tag="y_codes_in", bufs=3)
             nc.sync.dma_start(out=loads["y", c][:], in_=y_rows[c])
 
-        def widen_y(c, halves=(0, 1)):
-            if 0 in halves:
-                scaled["y", c] = work.tile([P, T * D], BF16, name="y_bf", tag="rows", bufs=2)
-            for h in halves:
-                cols = slice(2 * D * h, 2 * D * (h + 1))
-                nc.vector.tensor_tensor(
-                    out=scaled["y", c][:, cols], in0=loads["y", c][:, cols].bitcast(FP8), in1=scale_row[:], op=ALU.mult
-                )
+        def widen_y(c, copies=(nc.gpsimd.tensor_copy,)):
+            scaled["y", c] = work.tile([P, T * D], BF16, name="y_bf", tag="rows", bufs=2)
+            width = T * D // len(copies)
+            for h, copy in enumerate(copies):
+                cols = slice(width * h, width * (h + 1))
+                copy(out=scaled["y", c][:, cols], in_=loads["y", c][:, cols].bitcast(FP8))
 
         def turn(key, src, tag="turned"):
             words = src[:].bitcast(F32)
@@ -87,6 +84,17 @@ def tile_hsicexpkernelgrad_t_kernel(tc, x, u, y_bytes, y_scale, v, r, z, out):
             words = grouped[key][:].bitcast(F32).rearrange("p (n w) -> p n w", w=2)
             for h, copy in enumerate(halves):
                 copy(out=words[:, 2 * P * h : 2 * P * (h + 1), :], in_=banks[key, h][:].rearrange("p w n -> p n w"))
+
+        def group_y(c):
+            key = ("y", c)
+            grouped[key] = work.tile([P, T * CHUNK], BF16, name="grouped", tag="grouped", bufs=4, align_bytes=64)
+            for h in range(2):
+                nc.vector.tensor_tensor(
+                    out=grouped[key][:, 8 * P * h : 8 * P * (h + 1)].rearrange("p (n w e) -> p n w e", w=2, e=2),
+                    in0=banks[key, h][:].rearrange("p w n -> p (w n)").bitcast(BF16).rearrange("p (w n e) -> p n w e", w=2, e=2),
+                    in1=scale_in[:].rearrange("p (w e) -> p w e", w=2).unsqueeze(1).to_broadcast([P, 2 * P, 2, 2]),
+                    op=ALU.mult,
+                )
 
         def quantize(key, pool, tag, bufs):
             width = grouped[key].shape[1] // T
@@ -180,15 +188,20 @@ def tile_hsicexpkernelgrad_t_kernel(tc, x, u, y_bytes, y_scale, v, r, z, out):
         def combine(c):
             key = ("a", c)
             grouped[key] = work.tile([P, T * CHUNK], BF16, name="a_bf", tag="grouped", bufs=4, align_bytes=64)
-            mine = (CHUNK - (POOL_COLS if c < CHUNKS - 1 else 0)) // 4
-            parts = ((nc.gpsimd, slice(mine, CHUNK // 4)), (nc.vector, slice(0, mine)))
-            for engine, cols in parts[c // (CHUNKS - 1) :]:
-                engine.tensor_tensor(
-                    out=grouped[key][:].rearrange("p (n i t) -> p n t i", t=T, i=4)[:, cols],
-                    in0=lmat[c][:].rearrange("p t (n i) -> p n t i", i=4)[:, cols],
-                    in1=kmat[c][:].rearrange("p t (n i) -> p n t i", i=4)[:, cols],
+            mine = CHUNK - (POOL_COLS if c < CHUNKS - 1 else 0)
+            if mine < CHUNK:
+                nc.gpsimd.tensor_tensor(
+                    out=grouped[key][:, T * mine :].rearrange("p (n t) -> p n t", t=T),
+                    in0=lmat[c][:, :, mine:].rearrange("p t n -> p n t"),
+                    in1=kmat[c][:, :, mine:].rearrange("p t n -> p n t"),
                     op=ALU.mult,
                 )
+            nc.vector.tensor_tensor(
+                out=grouped[key][:, : T * mine].rearrange("p (n i t) -> p n t i", t=T, i=4),
+                in0=lmat[c][:, :, :mine].rearrange("p t (n i) -> p n t i", i=4),
+                in1=kmat[c][:, :, :mine].rearrange("p t (n i) -> p n t i", i=4),
+                op=ALU.mult,
+            )
 
         def product(c):
             code, scale = codes["a", c]
@@ -244,15 +257,6 @@ def tile_hsicexpkernelgrad_t_kernel(tc, x, u, y_bytes, y_scale, v, r, z, out):
             out=r_abs[:], in0=r_abs[:], scalar1=2.0**-120, scalar2=2.0**120, op0=ALU.max, op1=ALU.min
         )
 
-        scale_bank = psum.tile([P, T, P], F32, name="side", tag="side", bufs=2)
-        for t in range(T):
-            nc.tensor.transpose(scale_bank[:, t, :], scale_in[:, t : t + 1].to_broadcast([P, P]), ident[:])
-        for h in range(2):
-            nc.vector.tensor_copy(
-                out=scale_row[:, D * h : D * (h + 1)].rearrange("p (q t) -> p q t", t=T),
-                in_=scale_bank[:].rearrange("p t q -> p q t"),
-            )
-
         factors = keep.tile([P, 3, T], F32, name="factors")
         nc.vector.tensor_scalar(
             out=factors[:, 0, :], in0=r_abs[:], scalar1=2.0**-60, scalar2=2.0**60, op0=ALU.max, op1=ALU.min
@@ -273,43 +277,44 @@ def tile_hsicexpkernelgrad_t_kernel(tc, x, u, y_bytes, y_scale, v, r, z, out):
                 for t in range(T):
                     logits(("y", s), "v", t)
             if have(s + 2):
-                turn(("y", s + 2), scaled["y", s + 2])
+                group_y(s + 2)
             if 0 <= new_x < X_AHEAD:
                 turn(("x", new_x), loads["x", new_x], "side")
+            if have(s + 3):
+                turn(("y", s + 3), scaled["y", s + 3])
             if have(s):
                 exp_l(s)
-            if have(s + 2):
-                group(("y", s + 2))
+            if 0 <= new_x < X_AHEAD:
+                group(("x", new_x))
             if have(s + 1):
                 quantize(("y", s + 1), work, "w", 2)
             if 0 <= new_x - 1 < X_AHEAD:
                 quantize(("x", new_x - 1), work, "x", X_AHEAD + 1)
-            if have(s + 3):
-                widen_y(s + 3)
-            if 0 <= new_x < X_AHEAD:
-                copy = nc.scalar.copy if new_x < X_BOTH else nc.vector.tensor_copy
-                group(("x", new_x), (copy, nc.vector.tensor_copy))
-            if s + 4 < CHUNKS:
-                load_y(s + 4)
-            if 0 <= new_x + 2 < CHUNKS and new_x + 2 < X_AHEAD + 3:
+            if have(s + 4):
+                widen_y(s + 4)
+            if have(s + 5):
+                load_y(s + 5)
+            if 0 <= new_x + 2 < X_AHEAD + 2:
                 load_x(("x", new_x + 2), x_rows[new_x + 2])
 
-        widen_y(0)
-        turn("v", loads["v"])
-        group("v")
+        widen_y(0, (nc.vector.tensor_copy, nc.scalar.copy))
+        widen_y(1)
         turn(("y", 0), scaled["y", 0])
-        group(("y", 0))
-        widen_y(1, (0,))
-        quantize("v", keep, "v", 1)
-        quantize(("y", 0), work, "w", 2)
-        widen_y(1, (1,))
+        turn("v", loads["v"], "side")
+        group_y(0)
+        group("v")
         turn(("y", 1), scaled["y", 1])
-        group(("y", 1))
+        quantize(("y", 0), work, "w", 2)
+        quantize("v", keep, "v", 1)
+        group_y(1)
         widen_y(2)
+        turn(("y", 2), scaled["y", 2])
         load_y(3)
+        widen_y(3)
+        load_y(4)
         for s in range(CHUNKS):
             kernel_l_step(s)
-            if s == 1:
+            if s == CHUNKS - 4:
                 r_exp = keep.tile([P, T], F32, name="r_exp")
                 nc.gpsimd.tensor_tensor(out=r_log[:], in0=logs[:, 0, :], in1=logs[:, 1, :], op=ALU.add)
                 nc.gpsimd.tensor_tensor(out=r_log[:], in0=r_log[:], in1=logs[:, 2, :], op=ALU.add)
@@ -321,12 +326,12 @@ def tile_hsicexpkernelgrad_t_kernel(tc, x, u, y_bytes, y_scale, v, r, z, out):
                     out=r_sign[:], in0=r_in[:], scalar1=0.0, scalar2=2.0, op0=ALU.is_ge, op1=ALU.mult
                 )
                 nc.gpsimd.tensor_scalar(out=r_sign[:], in0=r_sign[:], scalar1=1.0, scalar2=None, op0=ALU.subtract)
-            if s == 2:
-                turn("u", loads["u"])
+            if s == 0:
+                turn("u", loads["u"], "side")
                 group("u")
-            if s == 3:
+            if s == 1:
                 quantize("u", keep, "u", 1)
-            if s == 4:
+            if s == CHUNKS - 2:
                 grouped["z"] = work.tile([P, Z * T], BF16, name="z_grouped", tag="grouped", bufs=4, align_bytes=64)
                 nc.vector.tensor_tensor(
                     out=grouped["z"][:].rearrange("p (n t) -> p n t", t=T),
@@ -334,7 +339,7 @@ def tile_hsicexpkernelgrad_t_kernel(tc, x, u, y_bytes, y_scale, v, r, z, out):
                     in1=r_sign[:].unsqueeze(1).to_broadcast([P, Z, T]),
                     op=ALU.mult,
                 )
-            if s == 5:
+            if s == CHUNKS - 1:
                 quantize("z", keep, "z", 1)
             if s >= CHUNKS - 3:
                 slot_sums(s - CHUNKS + 3)
@@ -366,7 +371,7 @@ def tile_hsicexpkernelgrad_t_kernel(tc, x, u, y_bytes, y_scale, v, r, z, out):
         spread_means(0)
         exp_k(0)
         spread_means(1)
-        if X_FIRST_STEP + X_AHEAD == CHUNKS:
+        if X_FIRST_STEP + X_AHEAD >= CHUNKS:
             quantize(("x", X_AHEAD - 1), work, "x", X_AHEAD + 1)
         reduce_rows(2)
         centre(0)

@@ -22,10 +22,10 @@ T = 4
 CHUNK = 512
 CHUNKS = N // CHUNK
 ROOT = 1.0 / math.sqrt(512.0)
-X_AHEAD = 14
-X_FIRST_STEP = 2
-X_BOTH = 11
-POOL_COLS = 208
+X_AHEAD = 3
+X_START = 13
+SUM_START = 1
+SUMS_AHEAD = 3
 
 
 def tile_hsicexpkernelgrad_t_kernel(tc, x, u, y_bytes, y_scale, v, r, z, out):
@@ -38,7 +38,6 @@ def tile_hsicexpkernelgrad_t_kernel(tc, x, u, y_bytes, y_scale, v, r, z, out):
         keep = ctx.enter_context(tc.tile_pool(name="keep", bufs=1))
         work = ctx.enter_context(tc.tile_pool(name="work", bufs=2))
         psum = ctx.enter_context(tc.psum_pool(name="psum", bufs=2))
-        ctx.enter_context(tc.manual_schedule())
 
         ident = keep.tile([P, P], F32, name="ident")
         scale_in = keep.tile([P, T], F32, name="scale_in")
@@ -50,7 +49,7 @@ def tile_hsicexpkernelgrad_t_kernel(tc, x, u, y_bytes, y_scale, v, r, z, out):
         col_sums = keep.tile([P, T, CHUNKS], F32, name="col_sums")
         row_means = keep.tile([P, T * CHUNKS], F32, name="row_means")
 
-        loads, scaled, grouped, codes, banks, lmat, kmat, outs = {}, {}, {}, {}, {}, {}, {}, {}
+        loads, scaled, grouped, codes, banks, lmat, kmat = {}, {}, {}, {}, {}, {}, {}
 
         def load_x(key, rows):
             loads[key] = work.tile([P, T * D], BF16, name="x_in", tag="x_in", bufs=3)
@@ -141,9 +140,11 @@ def tile_hsicexpkernelgrad_t_kernel(tc, x, u, y_bytes, y_scale, v, r, z, out):
                     bias=r_log[:, t : t + 1],
                 )
 
-        def slot_sums(c):
-            bank = psum.tile([P, T, P], F32, name="sums", tag="turned", bufs=2)
-            for b in range(T):
+        def slot_sums(c, tag="turned", blocks=range(T)):
+            if 0 in blocks:
+                banks["sums", c] = psum.tile([P, T, P], F32, name="sums", tag=tag, bufs=2)
+            bank = banks["sums", c]
+            for b in blocks:
                 for t in range(T):
                     nc.tensor.matmul(
                         bank[:, b, :],
@@ -153,10 +154,9 @@ def tile_hsicexpkernelgrad_t_kernel(tc, x, u, y_bytes, y_scale, v, r, z, out):
                         stop=(t == T - 1),
                         is_transpose=True,
                     )
-            banks["sums", c] = bank
 
-        def reduce_rows(c):
-            for b in range(T):
+        def reduce_rows(c, blocks=range(T)):
+            for b in blocks:
                 spare = work.tile([P, P], F32, name="spare", tag="spare", bufs=1)
                 nc.scalar.activation(
                     out=spare[:],
@@ -185,35 +185,29 @@ def tile_hsicexpkernelgrad_t_kernel(tc, x, u, y_bytes, y_scale, v, r, z, out):
                     op1=ALU.subtract,
                 )
 
-        def combine(c):
-            key = ("a", c)
-            grouped[key] = work.tile([P, T * CHUNK], BF16, name="a_bf", tag="grouped", bufs=4, align_bytes=64)
-            mine = CHUNK - (POOL_COLS if c < CHUNKS - 1 else 0)
-            if mine < CHUNK:
-                nc.gpsimd.tensor_tensor(
-                    out=grouped[key][:, T * mine :].rearrange("p (n t) -> p n t", t=T),
-                    in0=lmat[c][:, :, mine:].rearrange("p t n -> p n t"),
-                    in1=kmat[c][:, :, mine:].rearrange("p t n -> p n t"),
-                    op=ALU.mult,
-                )
+        def combine(c, h, parts):
+            key = ("a", c, h)
+            width = CHUNK // parts
+            cols = slice(width * h, width * (h + 1))
+            grouped[key] = work.tile([P, T * width], BF16, name="a_bf", tag="grouped", bufs=4, align_bytes=64)
             nc.vector.tensor_tensor(
-                out=grouped[key][:, : T * mine].rearrange("p (n i t) -> p n t i", t=T, i=4),
-                in0=lmat[c][:, :, :mine].rearrange("p t (n i) -> p n t i", i=4),
-                in1=kmat[c][:, :, :mine].rearrange("p t (n i) -> p n t i", i=4),
+                out=grouped[key][:].rearrange("p (n i t) -> p n t i", t=T, i=4),
+                in0=lmat[c][:, :, cols].rearrange("p t (n i) -> p n t i", i=4),
+                in1=kmat[c][:, :, cols].rearrange("p t (n i) -> p n t i", i=4),
                 op=ALU.mult,
             )
 
-        def product(c):
-            code, scale = codes["a", c]
+        def product(c, parts):
             z_code, z_scale = codes["z"]
             for h in range(2):
                 bank = psum.tile([P, 2, Z], F32, name="bank", tag="bank", bufs=4)
                 for b in range(2):
-                    cols = slice(P * (2 * h + b), P * (2 * h + b + 1))
+                    code, scale = codes["a", c, h * (parts - 1)]
+                    first = P * ((2 * h + b) % (T // parts))
                     nc.tensor.matmul_mx(
                         out=bank[:, b, :],
-                        lhsT=code[:, cols].bitcast(FP8X4),
-                        lhsT_scale=scale[:, cols],
+                        lhsT=code[:, first : first + P].bitcast(FP8X4),
+                        lhsT_scale=scale[:, first : first + P],
                         rhs=z_code[:].bitcast(FP8X4),
                         rhs_scale=z_scale[:],
                         start=True,
@@ -221,18 +215,24 @@ def tile_hsicexpkernelgrad_t_kernel(tc, x, u, y_bytes, y_scale, v, r, z, out):
                     )
                 banks["out", c, h] = bank
 
-        def finish(c):
-            outs[c] = work.tile([P, T * Z], F32, name="out_sb", tag="rows", bufs=2)
+        def finish(c, parts):
+            out_sb = work.tile([P, T * Z], F32, name="out_sb", tag="rows", bufs=2)
             for h in range(2):
-                nc.scalar.activation(
-                    out=outs[c][:, 2 * Z * h : 2 * Z * (h + 1)],
-                    in_=banks["out", c, h][:].rearrange("p b n -> p (b n)"),
-                    func=ACT.Copy,
-                    scale=ROOT,
-                )
+                cols = slice(2 * Z * h, 2 * Z * (h + 1))
+                bank = banks["out", c, h][:].rearrange("p b n -> p (b n)")
+                if h == parts - 1 == 1:
+                    nc.vector.tensor_scalar(
+                        out=out_sb[:, cols], in0=bank, scalar1=ROOT, scalar2=None, op0=ALU.mult
+                    )
+                else:
+                    nc.scalar.activation(out=out_sb[:, cols], in_=bank, func=ACT.Copy, scale=ROOT)
+            width = T * Z // parts
+            for h in range(parts):
+                cols = slice(width * h, width * (h + 1))
+                nc.sync.dma_start(out=out_rows[c][:, cols], in_=out_sb[:, cols])
 
-        def store(c):
-            nc.sync.dma_start(out=out_rows[c], in_=outs[c][:])
+        def parts_of(c):
+            return 2 if c == CHUNKS - 1 else 1
 
         def have(c):
             return 0 <= c < CHUNKS
@@ -272,24 +272,24 @@ def tile_hsicexpkernelgrad_t_kernel(tc, x, u, y_bytes, y_scale, v, r, z, out):
         nc.scalar.activation(out=one[:], in_=one[:], func=ACT.Exp)
 
         def kernel_l_step(s):
-            new_x = s - X_FIRST_STEP
+            new_x = s - X_START
             if have(s):
                 for t in range(T):
                     logits(("y", s), "v", t)
             if have(s + 2):
                 group_y(s + 2)
-            if 0 <= new_x < X_AHEAD:
-                turn(("x", new_x), loads["x", new_x], "side")
             if have(s + 3):
                 turn(("y", s + 3), scaled["y", s + 3])
+            if 0 <= new_x < X_AHEAD:
+                turn(("x", new_x), loads["x", new_x], "side")
             if have(s):
                 exp_l(s)
-            if 0 <= new_x < X_AHEAD:
-                group(("x", new_x))
             if have(s + 1):
                 quantize(("y", s + 1), work, "w", 2)
             if 0 <= new_x - 1 < X_AHEAD:
                 quantize(("x", new_x - 1), work, "x", X_AHEAD + 1)
+            if 0 <= new_x < X_AHEAD:
+                group(("x", new_x), (nc.scalar.copy, nc.vector.tensor_copy))
             if have(s + 4):
                 widen_y(s + 4)
             if have(s + 5):
@@ -297,7 +297,15 @@ def tile_hsicexpkernelgrad_t_kernel(tc, x, u, y_bytes, y_scale, v, r, z, out):
             if 0 <= new_x + 2 < X_AHEAD + 2:
                 load_x(("x", new_x + 2), x_rows[new_x + 2])
 
+        nc.gpsimd.tensor_scalar(
+            out=r_sign[:], in0=r_in[:], scalar1=0.0, scalar2=2.0, op0=ALU.is_ge, op1=ALU.mult
+        )
+        nc.gpsimd.tensor_scalar(out=r_sign[:], in0=r_sign[:], scalar1=1.0, scalar2=None, op0=ALU.subtract)
         widen_y(0, (nc.vector.tensor_copy, nc.scalar.copy))
+        nc.vector.tensor_tensor(out=r_log[:], in0=logs[:, 0, :], in1=logs[:, 1, :], op=ALU.add)
+        nc.vector.tensor_tensor(out=r_log[:], in0=r_log[:], in1=logs[:, 2, :], op=ALU.add)
+        r_exp = keep.tile([P, T], F32, name="r_exp")
+        nc.scalar.activation(out=r_exp[:], in_=r_log[:], func=ACT.Exp, scale=-1.0)
         widen_y(1)
         turn(("y", 0), scaled["y", 0])
         turn("v", loads["v"], "side")
@@ -306,7 +314,11 @@ def tile_hsicexpkernelgrad_t_kernel(tc, x, u, y_bytes, y_scale, v, r, z, out):
         turn(("y", 1), scaled["y", 1])
         quantize(("y", 0), work, "w", 2)
         quantize("v", keep, "v", 1)
+        nc.vector.tensor_tensor(out=r_exp[:], in0=r_exp[:], in1=r_abs[:], op=ALU.mult)
         group_y(1)
+        nc.vector.scalar_tensor_tensor(
+            out=r_log[:], in0=r_exp[:], scalar=-1.0, in1=r_log[:], op0=ALU.add, op1=ALU.add
+        )
         widen_y(2)
         turn(("y", 2), scaled["y", 2])
         load_y(3)
@@ -314,18 +326,6 @@ def tile_hsicexpkernelgrad_t_kernel(tc, x, u, y_bytes, y_scale, v, r, z, out):
         load_y(4)
         for s in range(CHUNKS):
             kernel_l_step(s)
-            if s == CHUNKS - 4:
-                r_exp = keep.tile([P, T], F32, name="r_exp")
-                nc.gpsimd.tensor_tensor(out=r_log[:], in0=logs[:, 0, :], in1=logs[:, 1, :], op=ALU.add)
-                nc.gpsimd.tensor_tensor(out=r_log[:], in0=r_log[:], in1=logs[:, 2, :], op=ALU.add)
-                nc.scalar.activation(out=r_exp[:], in_=r_log[:], func=ACT.Exp, scale=-1.0)
-                nc.gpsimd.tensor_tensor(out=r_exp[:], in0=r_exp[:], in1=r_abs[:], op=ALU.mult)
-                nc.gpsimd.tensor_scalar(out=r_exp[:], in0=r_exp[:], scalar1=1.0, scalar2=None, op0=ALU.subtract)
-                nc.gpsimd.tensor_tensor(out=r_log[:], in0=r_log[:], in1=r_exp[:], op=ALU.add)
-                nc.gpsimd.tensor_scalar(
-                    out=r_sign[:], in0=r_in[:], scalar1=0.0, scalar2=2.0, op0=ALU.is_ge, op1=ALU.mult
-                )
-                nc.gpsimd.tensor_scalar(out=r_sign[:], in0=r_sign[:], scalar1=1.0, scalar2=None, op0=ALU.subtract)
             if s == 0:
                 turn("u", loads["u"], "side")
                 group("u")
@@ -341,10 +341,11 @@ def tile_hsicexpkernelgrad_t_kernel(tc, x, u, y_bytes, y_scale, v, r, z, out):
                 )
             if s == CHUNKS - 1:
                 quantize("z", keep, "z", 1)
-            if s >= CHUNKS - 3:
-                slot_sums(s - CHUNKS + 3)
-            if s >= CHUNKS - 2:
-                reduce_rows(s - CHUNKS + 2)
+            block = s - SUM_START
+            if 0 <= block < T * SUMS_AHEAD:
+                slot_sums(block // T, "side", (block % T,))
+            if 0 < block <= T * SUMS_AHEAD:
+                reduce_rows((block - 1) // T, ((block - 1) % T,))
 
         col_mean = keep.tile([P, T], F32, name="col_mean")
         part_sum = keep.tile([P, 1], F32, name="part_sum")
@@ -371,42 +372,42 @@ def tile_hsicexpkernelgrad_t_kernel(tc, x, u, y_bytes, y_scale, v, r, z, out):
         spread_means(0)
         exp_k(0)
         spread_means(1)
-        if X_FIRST_STEP + X_AHEAD >= CHUNKS:
+        if X_START + X_AHEAD >= CHUNKS:
             quantize(("x", X_AHEAD - 1), work, "x", X_AHEAD + 1)
-        reduce_rows(2)
         centre(0)
 
         def kernel_k_step(s):
             if have(s + 1):
                 for t in range(T):
                     logits(("x", s + 1), "u", t)
-            if have(s - 2):
-                product(s - 2)
-            if have(s + 3) and s + 3 >= X_AHEAD:
-                turn(("x", s + 3), loads["x", s + 3])
-            if have(s + 3):
-                slot_sums(s + 3)
+            if have(s - 1):
+                product(s - 1, parts_of(s - 1))
+            if have(s + X_AHEAD):
+                turn(("x", s + X_AHEAD), loads["x", s + X_AHEAD])
+            if have(s + SUMS_AHEAD):
+                slot_sums(s + SUMS_AHEAD)
             if have(s + 2):
                 spread_means(s + 2)
             if have(s + 1):
                 exp_k(s + 1)
-            if have(s - 2):
-                finish(s - 2)
-                store(s - 2)
-            if have(s + 3) and s + 3 >= X_AHEAD:
-                group(("x", s + 3))
-            if have(s + 3):
-                reduce_rows(s + 3)
+            if have(s - 1):
+                finish(s - 1, parts_of(s - 1))
+            if have(s + X_AHEAD):
+                group(("x", s + X_AHEAD))
+            if have(s + SUMS_AHEAD):
+                reduce_rows(s + SUMS_AHEAD)
             if have(s + 1):
                 centre(s + 1)
             if have(s):
-                combine(s)
-            if have(s + 2) and s + 2 >= X_AHEAD:
-                quantize(("x", s + 2), work, "x", X_AHEAD + 1)
-            if have(s - 1):
-                quantize(("a", s - 1), work, "w", 2)
-            if have(s + 6) and s + 6 >= X_AHEAD + 3:
-                load_x(("x", s + 6), x_rows[s + 6])
+                for h in range(parts_of(s)):
+                    combine(s, h, parts_of(s))
+            if have(s + X_AHEAD - 1) and s > 0:
+                quantize(("x", s + X_AHEAD - 1), work, "x", X_AHEAD + 1)
+            if have(s):
+                for h in range(parts_of(s)):
+                    quantize(("a", s, h), work, "w", 2)
+            if have(s + X_AHEAD + 2):
+                load_x(("x", s + X_AHEAD + 2), x_rows[s + X_AHEAD + 2])
 
-        for s in range(CHUNKS + 2):
+        for s in range(CHUNKS + 1):
             kernel_k_step(s)

import math
from contextlib import ExitStack

import concourse.mybir as mybir
from concourse.masks import make_identity

N, M, D, Z = 8192, 512, 512, 256
FLOPS = 2 * N * M * (D + D + Z)

F32 = mybir.dt.float32
BF16 = mybir.dt.bfloat16
U32 = mybir.dt.uint32
U8 = mybir.dt.uint8
FP8 = mybir.dt.float8_e4m3fn
FP8X4 = mybir.dt.float8_e4m3fn_x4
ALU = mybir.AluOpType
ACT = mybir.ActivationFunctionType
AX = mybir.AxisListType

P = 128
T = 4
CHUNK = 512
CHUNKS = N // CHUNK
ROOT = 1.0 / math.sqrt(512.0)
X_AHEAD = 3
X_START = 13
SUM_START = 1
SUMS_AHEAD = 3


def tile_hsicexpkernelgrad_t_kernel(tc, x, u, y_bytes, y_scale, v, r, z, out):
    nc = tc.nc
    x_rows = x.rearrange("(c p b) k -> c p (b k)", p=P, b=T)
    y_rows = y_bytes.rearrange("(c p b) k -> c p (b k)", p=P, b=T)
    out_rows = out.rearrange("(c p b) n -> c p (b n)", p=P, b=T)

    with ExitStack() as ctx:
        keep = ctx.enter_context(tc.tile_pool(name="keep", bufs=1))
        work = ctx.enter_context(tc.tile_pool(name="work", bufs=2))
        psum = ctx.enter_context(tc.psum_pool(name="psum", bufs=2))

        ident = keep.tile([P, P], F32, name="ident")
        scale_in = keep.tile([P, T], F32, name="scale_in")
        r_in = keep.tile([P, T], BF16, name="r_in")
        r_abs = keep.tile([P, T], F32, name="r_abs")
        r_log = keep.tile([P, T], F32, name="r_log")
        r_sign = keep.tile([P, T], F32, name="r_sign")
        z_in = work.tile([P, T, Z], BF16, name="z_in", tag="x_in", bufs=3)
        col_sums = keep.tile([P, T, CHUNKS], F32, name="col_sums")
        row_means = keep.tile([P, T * CHUNKS], F32, name="row_means")

        loads, scaled, grouped, codes, banks, lmat, kmat = {}, {}, {}, {}, {}, {}, {}

        def load_x(key, rows):
            loads[key] = work.tile([P, T * D], BF16, name="x_in", tag="x_in", bufs=3)
            nc.sync.dma_start(out=loads[key][:], in_=rows)

        def load_y(c):
            loads["y", c] = work.tile([P, T * D], U8, name="y_codes_in", tag="y_codes_in", bufs=3)
            nc.sync.dma_start(out=loads["y", c][:], in_=y_rows[c])

        def widen_y(c, copies=(nc.gpsimd.tensor_copy,)):
            scaled["y", c] = work.tile([P, T * D], BF16, name="y_bf", tag="rows", bufs=2)
            width = T * D // len(copies)
            for h, copy in enumerate(copies):
                cols = slice(width * h, width * (h + 1))
                copy(out=scaled["y", c][:, cols], in_=loads["y", c][:, cols].bitcast(FP8))

        def turn(key, src, tag="turned"):
            words = src[:].bitcast(F32)
            for h in range(2):
                bank = psum.tile([P, 2, 2 * P], F32, name="turned", tag=tag, bufs=2)
                banks[key, h] = bank
                for b in (0, 1):
                    for w in range(2):
                        first = (2 * h + b) * (D // 2)
                        nc.tensor.transpose(
                            bank[:, w, P * b : P * (b + 1)], words[:, first + w : first + D // 2 : 2], ident[:]
                        )

        def group(key, halves=(nc.scalar.copy, nc.scalar.copy)):
            grouped[key] = work.tile([P, T * CHUNK], BF16, name="grouped", tag="grouped", bufs=4, align_bytes=64)
            words = grouped[key][:].bitcast(F32).rearrange("p (n w) -> p n w", w=2)
            for h, copy in enumerate(halves):
                copy(out=words[:, 2 * P * h : 2 * P * (h + 1), :], in_=banks[key, h][:].rearrange("p w n -> p n w"))

        def group_y(c):
            key = ("y", c)
            grouped[key] = work.tile([P, T * CHUNK], BF16, name="grouped", tag="grouped", bufs=4, align_bytes=64)
            for h in range(2):
                nc.vector.tensor_tensor(
                    out=grouped[key][:, 8 * P * h : 8 * P * (h + 1)].rearrange("p (n w e) -> p n w e", w=2, e=2),
                    in0=banks[key, h][:].rearrange("p w n -> p (w n)").bitcast(BF16).rearrange("p (w n e) -> p n w e", w=2, e=2),
                    in1=scale_in[:].rearrange("p (w e) -> p w e", w=2).unsqueeze(1).to_broadcast([P, 2 * P, 2, 2]),
                    op=ALU.mult,
                )

        def quantize(key, pool, tag, bufs):
            width = grouped[key].shape[1] // T
            code = pool.tile([P, width], U32, name="code" + tag, tag="code" + tag, bufs=bufs, align_bytes=64)
            scale = pool.tile([P, width], U8, name="scale" + tag, tag="scale" + tag, bufs=bufs, align_bytes=64)
            nc.vector.quantize_mx(out=code[:].bitcast(FP8X4), scales=scale[:], in_=grouped[key][:])
            codes[key] = (code, scale)

        def logits(key, weight, t):
            bank = psum.tile([P, CHUNK], F32, name="bank", tag="bank", bufs=4)
            w_code, w_scale = codes[weight]
            code, scale = codes[key]
            cols = slice(P * t, P * (t + 1))
            nc.tensor.matmul_mx(
                out=bank[:],
                lhsT=w_code[:, cols].bitcast(FP8X4),
                lhsT_scale=w_scale[:, cols],
                rhs=code[:].bitcast(FP8X4),
                rhs_scale=scale[:],
                start=True,
                stop=True,
            )
            banks[key, "logits", t] = bank

        def exp_l(c):
            lmat[c] = keep.tile([P, T, CHUNK], F32, name="l", tag="l", bufs=CHUNKS)
            for t in range(T):
                nc.scalar.activation(
                    out=lmat[c][:, t, :],
                    in_=banks[("y", c), "logits", t][:],
                    func=ACT.Exp,
                    scale=ROOT,
                    accum_out=col_sums[:, t, c : c + 1],
                )

        def exp_k(c):
            kmat[c] = work.tile([P, T, CHUNK], F32, name="k", tag="k", bufs=2)
            for t in range(T):
                nc.scalar.activation(
                    out=kmat[c][:, t, :],
                    in_=banks[("x", c), "logits", t][:],
                    func=ACT.Exp,
                    scale=ROOT,
                    bias=r_log[:, t : t + 1],
                )

        def slot_sums(c, tag="turned", blocks=range(T)):
            if 0 in blocks:
                banks["sums", c] = psum.tile([P, T, P], F32, name="sums", tag=tag, bufs=2)
            bank = banks["sums", c]
            for b in blocks:
                for t in range(T):
                    nc.tensor.matmul(
                        bank[:, b, :],
                        lhsT=lmat[c][:, t, P * b : P * (b + 1)],
                        rhs=ident[:],
                        start=(t == 0),
                        stop=(t == T - 1),
                        is_transpose=True,
                    )

        def reduce_rows(c, blocks=range(T)):
            for b in blocks:
                spare = work.tile([P, P], F32, name="spare", tag="spare", bufs=1)
                nc.scalar.activation(
                    out=spare[:],
                    in_=banks["sums", c][:, b, :],
                    func=ACT.Copy,
                    scale=1.0 / M,
                    accum_out=row_means[:, T * c + b : T * c + b + 1],
                )

        def spread_means(c):
            bank = psum.tile([P, T, P], F32, name="side", tag="side", bufs=2)
            for b in range(T):
                col = T * c + b
                nc.tensor.transpose(bank[:, b, :], row_means[:, col : col + 1].to_broadcast([P, P]), ident[:])
            banks["means", c] = bank

        def centre(c):
            means = banks["means", c][:].rearrange("p b i -> p (b i)")
            for t in range(T):
                nc.vector.scalar_tensor_tensor(
                    out=lmat[c][:, t, :],
                    in0=lmat[c][:, t, :],
                    scalar=col_shift[:, t : t + 1],
                    in1=means,
                    op0=ALU.add,
                    op1=ALU.subtract,
                )

        def combine(c, h, parts):
            key = ("a", c, h)
            width = CHUNK // parts
            cols = slice(width * h, width * (h + 1))
            grouped[key] = work.tile([P, T * width], BF16, name="a_bf", tag="grouped", bufs=4, align_bytes=64)
            nc.vector.tensor_tensor(
                out=grouped[key][:].rearrange("p (n i t) -> p n t i", t=T, i=4),
                in0=lmat[c][:, :, cols].rearrange("p t (n i) -> p n t i", i=4),
                in1=kmat[c][:, :, cols].rearrange("p t (n i) -> p n t i", i=4),
                op=ALU.mult,
            )

        def product(c, parts):
            z_code, z_scale = codes["z"]
            for h in range(2):
                bank = psum.tile([P, 2, Z], F32, name="bank", tag="bank", bufs=4)
                for b in range(2):
                    code, scale = codes["a", c, h * (parts - 1)]
                    first = P * ((2 * h + b) % (T // parts))
                    nc.tensor.matmul_mx(
                        out=bank[:, b, :],
                        lhsT=code[:, first : first + P].bitcast(FP8X4),
                        lhsT_scale=scale[:, first : first + P],
                        rhs=z_code[:].bitcast(FP8X4),
                        rhs_scale=z_scale[:],
                        start=True,
                        stop=True,
                    )
                banks["out", c, h] = bank

        def finish(c, parts):
            out_sb = work.tile([P, T * Z], F32, name="out_sb", tag="rows", bufs=2)
            for h in range(2):
                cols = slice(2 * Z * h, 2 * Z * (h + 1))
                bank = banks["out", c, h][:].rearrange("p b n -> p (b n)")
                if h == parts - 1 == 1:
                    nc.vector.tensor_scalar(
                        out=out_sb[:, cols], in0=bank, scalar1=ROOT, scalar2=None, op0=ALU.mult
                    )
                else:
                    nc.scalar.activation(out=out_sb[:, cols], in_=bank, func=ACT.Copy, scale=ROOT)
            width = T * Z // parts
            for h in range(parts):
                cols = slice(width * h, width * (h + 1))
                nc.sync.dma_start(out=out_rows[c][:, cols], in_=out_sb[:, cols])

        def parts_of(c):
            return 2 if c == CHUNKS - 1 else 1

        def have(c):
            return 0 <= c < CHUNKS

        nc.sync.dma_start(out=scale_in[:], in_=y_scale.rearrange("o (p t) -> p (o t)", t=T))
        nc.sync.dma_start(out=r_in[:], in_=r.rearrange("(p t) -> p t", t=T))
        load_y(0)
        load_x("v", v.rearrange("(p b) k -> p (b k)", b=T))
        load_y(1)
        load_y(2)
        load_x("u", u.rearrange("(p b) k -> p (b k)", b=T))
        nc.sync.dma_start(out=z_in[:], in_=z.rearrange("(p t) n -> p t n", t=T))
        one = keep.tile([P, 1], F32, name="one")
        nc.gpsimd.memset(one[:], 1.0)
        make_identity(nc, ident[:])
        nc.scalar.activation(out=one[:], in_=one[:], func=ACT.Ln)

        nc.vector.scalar_tensor_tensor(
            out=r_abs[:], in0=r_in[:], scalar=-1.0, in1=r_in[:], op0=ALU.mult, op1=ALU.max
        )
        nc.vector.tensor_scalar(
            out=r_abs[:], in0=r_abs[:], scalar1=2.0**-120, scalar2=2.0**120, op0=ALU.max, op1=ALU.min
        )

        factors = keep.tile([P, 3, T], F32, name="factors")
        nc.vector.tensor_scalar(
            out=factors[:, 0, :], in0=r_abs[:], scalar1=2.0**-60, scalar2=2.0**60, op0=ALU.max, op1=ALU.min
        )
        nc.vector.tensor_scalar(
            out=factors[:, 1, :], in0=r_abs[:], scalar1=2.0**-60, scalar2=1.0, op0=ALU.mult, op1=ALU.max
        )
        nc.vector.tensor_scalar(
            out=factors[:, 2, :], in0=r_abs[:], scalar1=2.0**60, scalar2=1.0, op0=ALU.mult, op1=ALU.min
        )
        logs = keep.tile([P, 3, T], F32, name="logs")
        nc.scalar.activation(out=logs[:], in_=factors[:], func=ACT.Ln)
        nc.scalar.activation(out=one[:], in_=one[:], func=ACT.Exp)

        def kernel_l_step(s):
            new_x = s - X_START
            if have(s):
                for t in range(T):
                    logits(("y", s), "v", t)
            if have(s + 2):
                group_y(s + 2)
            if have(s + 3):
                turn(("y", s + 3), scaled["y", s + 3])
            if 0 <= new_x < X_AHEAD:
                turn(("x", new_x), loads["x", new_x], "side")
            if have(s):
                exp_l(s)
            if have(s + 1):
                quantize(("y", s + 1), work, "w", 2)
            if 0 <= new_x - 1 < X_AHEAD:
                quantize(("x", new_x - 1), work, "x", X_AHEAD + 1)
            if 0 <= new_x < X_AHEAD:
                group(("x", new_x), (nc.scalar.copy, nc.vector.tensor_copy))
            if have(s + 4):
                widen_y(s + 4)
            if have(s + 5):
                load_y(s + 5)
            if 0 <= new_x + 2 < X_AHEAD + 2:
                load_x(("x", new_x + 2), x_rows[new_x + 2])

        nc.gpsimd.tensor_scalar(
            out=r_sign[:], in0=r_in[:], scalar1=0.0, scalar2=2.0, op0=ALU.is_ge, op1=ALU.mult
        )
        nc.gpsimd.tensor_scalar(out=r_sign[:], in0=r_sign[:], scalar1=1.0, scalar2=None, op0=ALU.subtract)
        widen_y(0, (nc.vector.tensor_copy, nc.scalar.copy))
        nc.vector.tensor_tensor(out=r_log[:], in0=logs[:, 0, :], in1=logs[:, 1, :], op=ALU.add)
        nc.vector.tensor_tensor(out=r_log[:], in0=r_log[:], in1=logs[:, 2, :], op=ALU.add)
        r_exp = keep.tile([P, T], F32, name="r_exp")
        nc.scalar.activation(out=r_exp[:], in_=r_log[:], func=ACT.Exp, scale=-1.0)
        widen_y(1)
        turn(("y", 0), scaled["y", 0])
        turn("v", loads["v"], "side")
        group_y(0)
        group("v")
        turn(("y", 1), scaled["y", 1])
        quantize(("y", 0), work, "w", 2)
        quantize("v", keep, "v", 1)
        nc.vector.tensor_tensor(out=r_exp[:], in0=r_exp[:], in1=r_abs[:], op=ALU.mult)
        group_y(1)
        nc.vector.scalar_tensor_tensor(
            out=r_log[:], in0=r_exp[:], scalar=-1.0, in1=r_log[:], op0=ALU.add, op1=ALU.add
        )
        widen_y(2)
        turn(("y", 2), scaled["y", 2])
        load_y(3)
        widen_y(3)
        load_y(4)
        for s in range(CHUNKS):
            kernel_l_step(s)
            if s == 0:
                turn("u", loads["u"], "side")
                group("u")
            if s == 1:
                quantize("u", keep, "u", 1)
            if s == CHUNKS - 2:
                grouped["z"] = work.tile([P, Z * T], BF16, name="z_grouped", tag="grouped", bufs=4, align_bytes=64)
                nc.vector.tensor_tensor(
                    out=grouped["z"][:].rearrange("p (n t) -> p n t", t=T),
                    in0=z_in[:].rearrange("p t n -> p n t"),
                    in1=r_sign[:].unsqueeze(1).to_broadcast([P, Z, T]),
                    op=ALU.mult,
                )
            if s == CHUNKS - 1:
                quantize("z", keep, "z", 1)
            block = s - SUM_START
            if 0 <= block < T * SUMS_AHEAD:
                slot_sums(block // T, "side", (block % T,))
            if 0 < block <= T * SUMS_AHEAD:
                reduce_rows((block - 1) // T, ((block - 1) % T,))

        col_mean = keep.tile([P, T], F32, name="col_mean")
        part_sum = keep.tile([P, 1], F32, name="part_sum")
        total = keep.tile([P, 1], F32, name="total")
        col_shift = keep.tile([P, T], F32, name="col_shift")
        nc.vector.tensor_reduce(out=part_sum[:], in_=col_sums[:], axis=AX.XY, op=ALU.add)
        nc.vector.tensor_reduce(out=col_mean[:], in_=col_sums[:], axis=AX.X, op=ALU.add)
        nc.vector.tensor_scalar(
            out=col_mean[:], in0=col_mean[:], scalar1=1.0 / N, scalar2=None, op0=ALU.mult
        )
        total_bank = psum.tile([P, P], F32, name="total_bank", tag="side", bufs=2)
        for t in range(T):
            logits(("x", 0), "u", t)
        nc.tensor.transpose(total_bank[:], part_sum[:].to_broadcast([P, P]), ident[:])
        nc.vector.tensor_reduce(out=total[:], in_=total_bank[:], axis=AX.X, op=ALU.add)
        nc.vector.scalar_tensor_tensor(
            out=col_shift[:],
            in0=total[:].to_broadcast([P, T]),
            scalar=1.0 / (N * M),
            in1=col_mean[:],
            op0=ALU.mult,
            op1=ALU.subtract,
        )
        spread_means(0)
        exp_k(0)
        spread_means(1)
        if X_START + X_AHEAD >= CHUNKS:
            quantize(("x", X_AHEAD - 1), work, "x", X_AHEAD + 1)
        centre(0)

        def kernel_k_step(s):
            if have(s + 1):
                for t in range(T):
                    logits(("x", s + 1), "u", t)
            if have(s - 1):
                product(s - 1, parts_of(s - 1))
            if have(s + X_AHEAD):
                turn(("x", s + X_AHEAD), loads["x", s + X_AHEAD])
            if have(s + SUMS_AHEAD):
                slot_sums(s + SUMS_AHEAD)
            if have(s + 2):
                spread_means(s + 2)
            if have(s + 1):
                exp_k(s + 1)
            if have(s - 1):
                finish(s - 1, parts_of(s - 1))
            if have(s + X_AHEAD):
                group(("x", s + X_AHEAD))
            if have(s + SUMS_AHEAD):
                reduce_rows(s + SUMS_AHEAD)
            if have(s + 1):
                centre(s + 1)
            if have(s):
                for h in range(parts_of(s)):
                    combine(s, h, parts_of(s))
            if have(s + X_AHEAD - 1) and s > 0:
                quantize(("x", s + X_AHEAD - 1), work, "x", X_AHEAD + 1)
            if have(s):
                for h in range(parts_of(s)):
                    quantize(("a", s, h), work, "w", 2)
            if have(s + X_AHEAD + 2):
                load_x(("x", s + X_AHEAD + 2), x_rows[s + X_AHEAD + 2])

        for s in range(CHUNKS + 1):
            kernel_k_step(s)
